import numpy as np
import ml_dtypes


def mxq(x, axis, fmt="e4m3"):
    dtype, down = {"e4m3": (ml_dtypes.float8_e4m3fn, 7), "e5m2": (ml_dtypes.float8_e5m2, 14)}[fmt]
    v = np.moveaxis(np.asarray(x, np.float32).astype(ml_dtypes.bfloat16).astype(np.float64), axis, -1)
    blocks = v.reshape(v.shape[:-1] + (-1, 32))
    amax = np.abs(blocks).max(-1, keepdims=True)
    byte = np.maximum(np.where(amax > 0, np.frexp(amax)[1] - 1 + 127, 0) - down, 1)
    scale = np.exp2(byte - 127.0)
    codes = (blocks / scale).astype(np.float32).astype(dtype).astype(np.float64)
    return np.moveaxis((codes * scale).reshape(v.shape), -1, axis)


WIDE = False


def mx_kscale(k):
    if not WIDE:
        return np.ones(k)
    levels = np.array([10, -10, 5, -5, 0])
    if k % 512:
        return np.exp2(np.random.permutation(np.resize(levels, k // 32))).repeat(32)
    a = np.empty((k // 512, 16))
    for p in range(k // 512):
        a[p, :8] = np.random.permutation(np.resize(levels, 8))
        for g in range(8):
            far = levels[np.abs(levels - a[p, g]) >= 10]
            a[p, g + 8] = far[np.random.randint(len(far))]
    return np.exp2(a.ravel()).repeat(32)


def f64(x):
    return np.asarray(x).astype(np.float64)


def striped(idx):
    return np.tile(idx.reshape(-1, 16).T, (8, 1)).astype(np.uint16)


def unstriped(offs):
    return offs[:16].T.reshape(-1).astype(np.int64)


def pack_weight(w):
    k, n = w.shape
    w = f64(np.asarray(w, np.float32).astype(ml_dtypes.bfloat16)).reshape(k // 32, 32, n)
    amax = np.abs(w).max(1)
    byte = np.clip(np.where(amax > 0, np.frexp(amax)[1] - 1 + 127 - 7, 1), 1, 254)
    scaled = (w * np.exp2(127.0 - byte)[:, None, :]).reshape(k, n).astype(np.float32)
    words = np.ascontiguousarray(scaled.reshape(k // 512, 128, 4, n).transpose(0, 1, 3, 2)).astype(ml_dtypes.float8_e4m3fn).view(np.uint8)
    return words, np.ascontiguousarray(byte.astype(np.uint8).reshape(k // 512, 16, n))


def unpack_weight(words, scales):
    g, p, n, _ = words.shape
    vals = np.ascontiguousarray(words).view(ml_dtypes.float8_e4m3fn).astype(np.float64) * np.repeat(np.exp2(scales.astype(np.float64) - 127.0), 8, axis=1)[..., None]
    return vals.transpose(0, 1, 3, 2).reshape(g * 512, n)


def relu(v):
    return np.maximum(v, 0.0)


K, T, S, H, N = 1024, 4096, 1024, 512, 256


def setup_inputs():
    n = np.random.standard_normal
    s = mx_kscale(K)[:, None]
    u = mx_kscale(H)
    packed_xT = pack_weight(n((K, T)) * s)
    return {
        "x_words": packed_xT[0],
        "x_scales": packed_xT[1],
        "w1": (n((K, H)) / np.sqrt(K) / s * u).astype(np.float32),
        "r1": (n((K, H)) / np.sqrt(K) / s * u).astype(np.float32),
        "w2": (n((H, N)) / np.sqrt(H) / u[:, None]).astype(np.float32),
        "r2": (n((H, N)) / np.sqrt(H) / u[:, None]).astype(np.float32),
        "inv": (np.random.uniform(0.5, 1.5, (N, 1))).astype(np.float32),
        "capv": (np.random.uniform(1.0, 5.0, (N, S))).astype(np.float32),
        "offs": striped(np.random.permutation(T)[:S]),
    }


def reference(x_words, x_scales, w1, r1, w2, r2, inv, capv, offs):
    xq = unpack_weight(x_words, x_scales)[:, unstriped(offs)]
    h = relu(mxq(f64(w1), 0, "e4m3").T @ xq)
    gg = relu(mxq(f64(r1), 0, "e4m3").T @ xq)
    y = mxq(f64(r2), 0, "e4m3").T @ mxq(gg, 0, "e4m3")
    dd = (mxq(f64(w2), 0, "e4m3").T @ mxq(h, 0, "e4m3")) - y
    return np.minimum((f64(inv) * dd) ** 2, f64(capv))

@@ -1,0 +1,206 @@
+from contextlib import ExitStack
+
+import concourse.mybir as mybir
+
+K, T, S, H, N = 1024, 4096, 1024, 512, 256
+FLOPS = 2 * S * (2 * K * H + 2 * H * N)
+
+F32 = mybir.dt.float32
+BF16 = mybir.dt.bfloat16
+I32 = mybir.dt.int32
+U32 = mybir.dt.uint32
+U16 = mybir.dt.uint16
+U8 = mybir.dt.uint8
+FP8X4 = mybir.dt.float8_e4m3fn_x4
+ACT = mybir.ActivationFunctionType
+ALU = mybir.AluOpType
+
+P = 128
+PACK = 4
+PASSES = K // (P * PACK)
+BLOCK = 128
+H_CHUNK = 512
+LAG = 2
+SCALAR_SECOND = {"w2"}
+OUT_CHUNKS = [256,256,256,128,128]
+SCALAR_CASTS = {("w1", 1, 1)}
+VECTOR_RELUS = {("r1", 3), ("r1", 6)}
+
+
+def tile_picked_yrnd_norm_p_kernel(
+    tc, x_words, x_scales, w1, r1, w2, r2, inv, capv, offs, out
+):
+    nc = tc.nc
+    with ExitStack() as ctx:
+        keep = ctx.enter_context(tc.tile_pool(name="keep", bufs=1))
+        psum = ctx.enter_context(tc.psum_pool(name="psum", bufs=8))
+
+        def tile(shape, dtype, name):
+            return keep.tile(shape, dtype, name=name, align_bytes=64)
+
+        offsets = keep.tile([P, S // 16], U16, name="offsets")
+        nc.sync.dma_start(offsets[:], offs)
+
+        scale_table = tile([P, T], U8, "scale_table")
+        nc.vector.memset(scale_table[:].bitcast(I32), 0)
+
+        raw1 = {}
+        word_tables = []
+
+        def load_first(name, w, o):
+            raw = tile([P, PACK, H], F32, "raw_%s_%d" % (name, o))
+            nc.sync.dma_start(out=raw[:], in_=w[o * 512 : (o + 1) * 512, :].rearrange("(p j) c -> p j c", j=PACK))
+            raw1[(name, o)] = raw
+
+        def load_words(o):
+            table = tile([P, T], I32, "word_table%d" % o)
+            nc.sync.dma_start(out=table[:], in_=x_words[o].rearrange("p c r -> p (c r)").bitcast(I32))
+            word_tables.append(table)
+
+        load_first("w1", w1, 1)
+        for so in range(PASSES):
+            for q in range(4):
+                nc.sync.dma_start(
+                    out=scale_table[32 * q + 4 * so : 32 * q + 4 * so + 4, :].bitcast(I32),
+                    in_=x_scales[so, 4 * q : 4 * q + 4, :].bitcast(I32),
+                )
+        load_words(0)
+        load_first("w1", w1, 0)
+        load_words(1)
+        load_first("r1", r1, 0)
+        load_first("r1", r1, 1)
+        raw2 = {}
+        for name, w in (("w2", w2), ("r2", r2)):
+            raw = tile([P, PACK, N], F32, "raw_%s" % name)
+            rows = w.rearrange("(b u q e) n -> u b q (e n)", u=2, q=8, e=2)
+            for u in range(2):
+                nc.sync.dma_start(out=raw[:, 2 * u : 2 * u + 2, :].rearrange("p e n -> p (e n)"), in_=rows[u])
+            raw2[name] = raw
+        inv_sb = tile([P, 2], F32, "inv_sb")
+        with nc.allow_non_contiguous_dma(reason="one factor for each output row"):
+            nc.sync.dma_start(out=inv_sb[:], in_=inv.rearrange("(m p) u -> p (m u)", p=P))
+        cap_sb = []
+        for half in range(2):
+            cap = tile([P, 2, 512], F32, "cap%d" % half)
+            nc.sync.dma_start(out=cap[:], in_=capv.rearrange("(m p) j -> p m j", p=P)[:, :, half * 512 : (half + 1) * 512])
+            cap_sb.append(cap)
+
+        x_plane = tile([P, S], U8, "x_plane")
+        nc.vector.tensor_copy(out=x_plane[:], in_=scale_table[:].indirect(offsets[:]))
+        x_codes = {}
+        for o in range(PASSES):
+            for half in range(2):
+                codes = tile([P, 512], U32, "x_codes%d_%d" % (o, half))
+                nc.vector.tensor_copy(
+                    out=codes[:], in_=word_tables[o][:].bitcast(U32).indirect(offsets[:, 32 * half : 32 * half + 32])
+                )
+                x_codes[(o, half)] = codes
+
+        def quantize(grouped, width, name):
+            codes = tile([P, width], U32, name + "_codes")
+            plane = tile([P, width], U8, name + "_plane")
+            nc.vector.quantize_mx(out=codes[:].bitcast(FP8X4), scales=plane[:], in_=grouped)
+            return codes, plane
+
+        def first_weights(name, o):
+            grouped = []
+            for u in range(2):
+                g = tile([P, 2, 16, 8, PACK], BF16, "g_%s_%d_%d" % (name, o, u))
+                src = raw1[(name, o)][:].rearrange("p j (b u q e) -> p u b q e j", u=2, q=8, e=2)[:, u]
+                dst = g[:].rearrange("p e b q j -> p b q e j")
+                if (name, o, u) in SCALAR_CASTS:
+                    for e in range(2):
+                        nc.scalar.activation(out=dst[:, :, :, e, :], in_=src[:, :, :, e, :], func=ACT.Copy)
+                else:
+                    nc.vector.tensor_copy(out=dst, in_=src)
+                grouped.append(g)
+            slots = []
+            for u in range(2):
+                codes, plane = quantize(
+                    grouped[u][:].rearrange("p e b q j -> p (e b q j)"), 2 * P, "q_%s_%d_%d" % (name, o, u)
+                )
+                for e in range(2):
+                    slots.append((codes[:, e * P : (e + 1) * P], plane[:, e * P : (e + 1) * P]))
+            return slots
+
+        def second_weights(name, sign):
+            g = tile([P, N, PACK], BF16, "g_%s" % name)
+            src = raw2[name][:].rearrange("p t n -> p n t")
+            if name in SCALAR_SECOND:
+                nc.scalar.activation(out=g[:], in_=src, func=ACT.Copy, scale=sign)
+            else:
+                nc.vector.tensor_scalar(out=g[:], in0=src, scalar1=sign, scalar2=None, op0=ALU.mult)
+            return quantize(g[:].rearrange("p n t -> p (n t)"), N, "q_%s" % name)
+
+        def hidden_pass(acc, slots, o, block):
+            half, col = divmod(block * BLOCK, 512)
+            for t in range(PACK):
+                codes, plane = slots[t]
+                nc.tensor.matmul_mx(
+                    out=acc[:, t * BLOCK : (t + 1) * BLOCK],
+                    lhsT=codes.bitcast(FP8X4),
+                    lhsT_scale=plane,
+                    rhs=x_codes[(o, half)][:, col : col + BLOCK].bitcast(FP8X4),
+                    rhs_scale=x_plane[4 * o : P, block * BLOCK : (block + 1) * BLOCK],
+                    start=(o == 0 and t == 0),
+                    stop=(o == PASSES - 1 and t == PACK - 1),
+                )
+
+        def hidden_chunk(name, weights, start, width):
+            grouped = tile([P, width, PACK], BF16, "hid_%s_%d" % (name, start))
+            for n0 in range(0, width, BLOCK):
+                block = (start + n0) // BLOCK
+                acc = psum.tile([P, 512], F32, name="bank")
+                for o in range(PASSES):
+                    hidden_pass(acc, weights[o], o, block)
+                src = acc[:].rearrange("p (t n) -> p n t", t=PACK)
+                dst = grouped[:, n0 : n0 + BLOCK, :]
+                if (name, block) in VECTOR_RELUS:
+                    nc.vector.tensor_scalar(out=dst, in0=src, scalar1=0.0, scalar2=None, op0=ALU.max)
+                else:
+                    nc.scalar.activation(out=dst, in_=src, func=ACT.Relu)
+            return quantize(grouped[:].rearrange("p n t -> p (n t)"), width, "q_hid_%s_%d" % (name, start))
+
+        w1_q = [first_weights("w1", o) for o in range(PASSES)]
+        r1_q = [first_weights("r1", o) for o in range(PASSES)]
+        h_q = [hidden_chunk("w1", w1_q, start, H_CHUNK) for start in range(0, S, H_CHUNK)]
+        w2_q = second_weights("w2", 1.0)
+        r2_q = second_weights("r2", -1.0)
+
+        out_view = out.rearrange("(m p) j -> p m j", p=P)
+
+        def output_chunk(start, width, g_codes, g_plane):
+            h_codes, h_plane = h_q[start // H_CHUNK]
+            h_cols = slice(start % H_CHUNK, start % H_CHUNK + width)
+            acc = psum.tile([P, 512], F32, name="bank")
+            squared = tile([P, 2, width], F32, "squared%d" % start)
+            products = ((w2_q, h_codes[:, h_cols], h_plane[:, h_cols]), (r2_q, g_codes[:], g_plane[:]))
+            for i, (weights, codes, plane) in enumerate(products):
+                for m in range(2):
+                    rows = slice(m * P, (m + 1) * P)
+                    nc.tensor.matmul_mx(
+                        out=acc[:, m * width : (m + 1) * width],
+                        lhsT=weights[0][:, rows].bitcast(FP8X4),
+                        lhsT_scale=weights[1][:, rows],
+                        rhs=codes.bitcast(FP8X4),
+                        rhs_scale=plane,
+                        start=(i == 0 and m == 0),
+                        stop=(i == 1 and m == 1),
+                    )
+            for m in range(2):
+                nc.scalar.activation(
+                    out=squared[:, m, :], in_=acc[:, m * width : (m + 1) * width], func=ACT.Square, scale=inv_sb[:, m : m + 1]
+                )
+            result = tile([P, 2, width], F32, "result%d" % start)
+            nc.vector.tensor_tensor(
+                out=result[:], in0=squared[:], in1=cap_sb[start // 512][:, :, start % 512 : start % 512 + width], op=ALU.min
+            )
+            nc.sync.dma_start(out=out_view[:, :, start : start + width], in_=result[:])
+
+        starts = [sum(OUT_CHUNKS[:i]) for i in range(len(OUT_CHUNKS))]
+        g_q = []
+        for i in range(len(OUT_CHUNKS) + LAG):
+            if i < len(OUT_CHUNKS):
+                g_q.append(hidden_chunk("r1", r1_q, starts[i], OUT_CHUNKS[i]))
+            if i >= LAG:
+                output_chunk(starts[i - LAG], OUT_CHUNKS[i - LAG], *g_q[i - LAG])

@@ -43,6 +43,12 @@ def tile_picked_yrnd_norm_p_kernel(
 
         scale_table = tile([P, T], U8, "scale_table")
         nc.vector.memset(scale_table[:].bitcast(I32), 0)
+        nc.scalar.dma_start(
+            out=scale_table[0:P:4, :].bitcast(I32),
+            in_=x_scales.rearrange("o q c -> (o q) c").bitcast(I32),
+        )
+        x_plane = tile([P, S], U8, "x_plane")
+        nc.vector.memset(x_plane[:].bitcast(I32), 0)
 
         raw1 = {}
         word_tables = []
@@ -58,12 +64,6 @@ def tile_picked_yrnd_norm_p_kernel(
             word_tables.append(table)
 
         load_first("w1", w1, 1)
-        for so in range(PASSES):
-            for q in range(4):
-                nc.sync.dma_start(
-                    out=scale_table[32 * q + 4 * so : 32 * q + 4 * so + 4, :].bitcast(I32),
-                    in_=x_scales[so, 4 * q : 4 * q + 4, :].bitcast(I32),
-                )
         load_words(0)
         load_first("w1", w1, 0)
         load_words(1)
@@ -85,8 +85,14 @@ def tile_picked_yrnd_norm_p_kernel(
             nc.sync.dma_start(out=cap[:], in_=capv.rearrange("(m p) j -> p m j", p=P)[:, :, half * 512 : (half + 1) * 512])
             cap_sb.append(cap)
 
-        x_plane = tile([P, S], U8, "x_plane")
-        nc.vector.tensor_copy(out=x_plane[:], in_=scale_table[:].indirect(offsets[:]))
+        picked_scales = tile([P, S], U8, "picked_scales")
+        nc.vector.tensor_copy(out=picked_scales[:], in_=scale_table[:].indirect(offsets[:]))
+        for o in range(PASSES):
+            for r in range(4):
+                nc.scalar.dma_start(
+                    out=x_plane[4 * o + r : P : 32, :].bitcast(I32),
+                    in_=picked_scales[64 * o + 4 * r : 64 * o + 64 : 16, :].bitcast(I32),
+                )
         x_codes = {}
         for o in range(PASSES):
             for half in range(2):

@@ -19,12 +19,12 @@ P = 128
 PACK = 4
 PASSES = K // (P * PACK)
 BLOCK = 128
-H_CHUNK = 512
-LAG = 2
+H_CHUNK = 1024
+LAG = 3
 SCALAR_SECOND = {"w2"}
-OUT_CHUNKS = [256,256,256,128,128]
+OUT_CHUNKS = [256,256,256,256]
 SCALAR_CASTS = {("w1", 1, 1)}
-VECTOR_RELUS = {("r1", 3), ("r1", 6)}
+VECTOR_RELUS = {("r1", 2), ("r1", 5)}
 
 
 def tile_picked_yrnd_norm_p_kernel(
@@ -35,20 +35,17 @@ def tile_picked_yrnd_norm_p_kernel(
         keep = ctx.enter_context(tc.tile_pool(name="keep", bufs=1))
         psum = ctx.enter_context(tc.psum_pool(name="psum", bufs=8))
 
-        def tile(shape, dtype, name):
-            return keep.tile(shape, dtype, name=name, align_bytes=64)
+        def tile(shape, dtype, name, tag=None):
+            return keep.tile(shape, dtype, name=name, tag=tag or name, align_bytes=64)
 
         offsets = keep.tile([P, S // 16], U16, name="offsets")
         nc.sync.dma_start(offsets[:], offs)
 
         scale_table = tile([P, T], U8, "scale_table")
         nc.vector.memset(scale_table[:].bitcast(I32), 0)
-        nc.scalar.dma_start(
-            out=scale_table[0:P:4, :].bitcast(I32),
-            in_=x_scales.rearrange("o q c -> (o q) c").bitcast(I32),
-        )
-        x_plane = tile([P, S], U8, "x_plane")
-        nc.vector.memset(x_plane[:].bitcast(I32), 0)
+        x_planes = [tile([P, S], U8, "x_plane%d" % o) for o in range(PASSES)]
+        for plane in x_planes:
+            nc.vector.memset(plane[:].bitcast(I32), 0)
 
         raw1 = {}
         word_tables = []
@@ -63,10 +60,25 @@ def tile_picked_yrnd_norm_p_kernel(
             nc.sync.dma_start(out=table[:], in_=x_words[o].rearrange("p c r -> p (c r)").bitcast(I32))
             word_tables.append(table)
 
+        def move_scales(o):
+            for r in range(4):
+                nc.sync.dma_start(
+                    out=x_planes[o][r:P:32, :].bitcast(I32),
+                    in_=picked_scales[64 * o + 4 * r : 64 * o + 64 : 16, :].bitcast(I32),
+                )
+
         load_first("w1", w1, 1)
+        nc.sync.dma_start(
+            out=scale_table[0:P:4, :].bitcast(I32),
+            in_=x_scales.rearrange("o q c -> (o q) c").bitcast(I32),
+        )
         load_words(0)
         load_first("w1", w1, 0)
+        picked_scales = tile([P, S], U8, "picked_scales")
+        nc.vector.tensor_copy(out=picked_scales[:], in_=scale_table[:].indirect(offsets[:]))
+        move_scales(0)
         load_words(1)
+        move_scales(1)
         load_first("r1", r1, 0)
         load_first("r1", r1, 1)
         raw2 = {}
@@ -85,14 +97,6 @@ def tile_picked_yrnd_norm_p_kernel(
             nc.sync.dma_start(out=cap[:], in_=capv.rearrange("(m p) j -> p m j", p=P)[:, :, half * 512 : (half + 1) * 512])
             cap_sb.append(cap)
 
-        picked_scales = tile([P, S], U8, "picked_scales")
-        nc.vector.tensor_copy(out=picked_scales[:], in_=scale_table[:].indirect(offsets[:]))
-        for o in range(PASSES):
-            for r in range(4):
-                nc.scalar.dma_start(
-                    out=x_plane[4 * o + r : P : 32, :].bitcast(I32),
-                    in_=picked_scales[64 * o + 4 * r : 64 * o + 64 : 16, :].bitcast(I32),
-                )
         x_codes = {}
         for o in range(PASSES):
             for half in range(2):
@@ -102,8 +106,8 @@ def tile_picked_yrnd_norm_p_kernel(
                 )
                 x_codes[(o, half)] = codes
 
-        def quantize(grouped, width, name):
-            codes = tile([P, width], U32, name + "_codes")
+        def quantize(grouped, width, name, tag=None):
+            codes = tile([P, width], U32, name + "_codes", tag)
             plane = tile([P, width], U8, name + "_plane")
             nc.vector.quantize_mx(out=codes[:].bitcast(FP8X4), scales=plane[:], in_=grouped)
             return codes, plane
@@ -147,12 +151,12 @@ def tile_picked_yrnd_norm_p_kernel(
                     lhsT=codes.bitcast(FP8X4),
                     lhsT_scale=plane,
                     rhs=x_codes[(o, half)][:, col : col + BLOCK].bitcast(FP8X4),
-                    rhs_scale=x_plane[4 * o : P, block * BLOCK : (block + 1) * BLOCK],
+                    rhs_scale=x_planes[o][:, block * BLOCK : (block + 1) * BLOCK],
                     start=(o == 0 and t == 0),
                     stop=(o == PASSES - 1 and t == PACK - 1),
                 )
 
-        def hidden_chunk(name, weights, start, width):
+        def hidden_chunk(name, weights, start, width, tag=None):
             grouped = tile([P, width, PACK], BF16, "hid_%s_%d" % (name, start))
             for n0 in range(0, width, BLOCK):
                 block = (start + n0) // BLOCK
@@ -165,11 +169,11 @@ def tile_picked_yrnd_norm_p_kernel(
                     nc.vector.tensor_scalar(out=dst, in0=src, scalar1=0.0, scalar2=None, op0=ALU.max)
                 else:
                     nc.scalar.activation(out=dst, in_=src, func=ACT.Relu)
-            return quantize(grouped[:].rearrange("p n t -> p (n t)"), width, "q_hid_%s_%d" % (name, start))
+            return quantize(grouped[:].rearrange("p n t -> p (n t)"), width, "q_hid_%s_%d" % (name, start), tag)
 
         w1_q = [first_weights("w1", o) for o in range(PASSES)]
         r1_q = [first_weights("r1", o) for o in range(PASSES)]
-        h_q = [hidden_chunk("w1", w1_q, start, H_CHUNK) for start in range(0, S, H_CHUNK)]
+        h_q = [hidden_chunk("w1", w1_q, start, H_CHUNK, "raw_r1_1") for start in range(0, S, H_CHUNK)]
         w2_q = second_weights("w2", 1.0)
         r2_q = second_weights("r2", -1.0)
 

@@ -88,14 +88,11 @@ def tile_picked_yrnd_norm_p_kernel(
             for u in range(2):
                 nc.sync.dma_start(out=raw[:, 2 * u : 2 * u + 2, :].rearrange("p e n -> p (e n)"), in_=rows[u])
             raw2[name] = raw
+        cap_sb = tile([P, 2, S], F32, "cap_sb")
+        nc.sync.dma_start(out=cap_sb[:], in_=capv.rearrange("(m p) j -> p m j", p=P))
         inv_sb = tile([P, 2], F32, "inv_sb")
         with nc.allow_non_contiguous_dma(reason="one factor for each output row"):
             nc.sync.dma_start(out=inv_sb[:], in_=inv.rearrange("(m p) u -> p (m u)", p=P))
-        cap_sb = []
-        for half in range(2):
-            cap = tile([P, 2, 512], F32, "cap%d" % half)
-            nc.sync.dma_start(out=cap[:], in_=capv.rearrange("(m p) j -> p m j", p=P)[:, :, half * 512 : (half + 1) * 512])
-            cap_sb.append(cap)
 
         x_codes = {}
         for o in range(PASSES):
@@ -135,11 +132,12 @@ def tile_picked_yrnd_norm_p_kernel(
 
         def second_weights(name, sign):
             g = tile([P, N, PACK], BF16, "g_%s" % name)
-            src = raw2[name][:].rearrange("p t n -> p n t")
+            src = raw2[name][:].rearrange("p t (c i) -> p c t i", i=4)
+            dst = g[:].rearrange("p (c i) t -> p c t i", i=4)
             if name in SCALAR_SECOND:
-                nc.scalar.activation(out=g[:], in_=src, func=ACT.Copy, scale=sign)
+                nc.scalar.activation(out=dst, in_=src, func=ACT.Copy, scale=sign)
             else:
-                nc.vector.tensor_scalar(out=g[:], in0=src, scalar1=sign, scalar2=None, op0=ALU.mult)
+                nc.vector.tensor_scalar(out=dst, in0=src, scalar1=sign, scalar2=None, op0=ALU.mult)
             return quantize(g[:].rearrange("p n t -> p (n t)"), N, "q_%s" % name)
 
         def hidden_pass(acc, slots, o, block):
@@ -177,13 +175,11 @@ def tile_picked_yrnd_norm_p_kernel(
         w2_q = second_weights("w2", 1.0)
         r2_q = second_weights("r2", -1.0)
 
-        out_view = out.rearrange("(m p) j -> p m j", p=P)
 
         def output_chunk(start, width, g_codes, g_plane):
             h_codes, h_plane = h_q[start // H_CHUNK]
             h_cols = slice(start % H_CHUNK, start % H_CHUNK + width)
             acc = psum.tile([P, 512], F32, name="bank")
-            squared = tile([P, 2, width], F32, "squared%d" % start)
             products = ((w2_q, h_codes[:, h_cols], h_plane[:, h_cols]), (r2_q, g_codes[:], g_plane[:]))
             for i, (weights, codes, plane) in enumerate(products):
                 for m in range(2):
@@ -198,14 +194,15 @@ def tile_picked_yrnd_norm_p_kernel(
                         stop=(i == 1 and m == 1),
                     )
             for m in range(2):
+                squared = tile([P, width], F32, "squared%d_%d" % (start, m))
                 nc.scalar.activation(
-                    out=squared[:, m, :], in_=acc[:, m * width : (m + 1) * width], func=ACT.Square, scale=inv_sb[:, m : m + 1]
+                    out=squared[:], in_=acc[:, m * width : (m + 1) * width], func=ACT.Square, scale=inv_sb[:, m : m + 1]
                 )
-            result = tile([P, 2, width], F32, "result%d" % start)
-            nc.vector.tensor_tensor(
-                out=result[:], in0=squared[:], in1=cap_sb[start // 512][:, :, start % 512 : start % 512 + width], op=ALU.min
-            )
-            nc.sync.dma_start(out=out_view[:, :, start : start + width], in_=result[:])
+                result = tile([P, width], F32, "result%d_%d" % (start, m))
+                nc.vector.tensor_tensor(
+                    out=result[:], in0=squared[:], in1=cap_sb[:, m, start : start + width], op=ALU.min
+                )
+                nc.sync.dma_start(out=out[m * P : (m + 1) * P, start : start + width], in_=result[:])
 
         starts = [sum(OUT_CHUNKS[:i]) for i in range(len(OUT_CHUNKS))]
         g_q = []

@@ -88,11 +88,11 @@ def tile_picked_yrnd_norm_p_kernel(
             for u in range(2):
                 nc.sync.dma_start(out=raw[:, 2 * u : 2 * u + 2, :].rearrange("p e n -> p (e n)"), in_=rows[u])
             raw2[name] = raw
-        cap_sb = tile([P, 2, S], F32, "cap_sb")
-        nc.sync.dma_start(out=cap_sb[:], in_=capv.rearrange("(m p) j -> p m j", p=P))
         inv_sb = tile([P, 2], F32, "inv_sb")
         with nc.allow_non_contiguous_dma(reason="one factor for each output row"):
             nc.sync.dma_start(out=inv_sb[:], in_=inv.rearrange("(m p) u -> p (m u)", p=P))
+        cap_sb = tile([P, 2, S], F32, "cap_sb")
+        nc.sync.dma_start(out=cap_sb[:], in_=capv.rearrange("(m p) j -> p m j", p=P))
 
         x_codes = {}
         for o in range(PASSES):
@@ -119,7 +119,8 @@ def tile_picked_yrnd_norm_p_kernel(
                     for e in range(2):
                         nc.scalar.activation(out=dst[:, :, :, e, :], in_=src[:, :, :, e, :], func=ACT.Copy)
                 else:
-                    nc.vector.tensor_copy(out=dst, in_=src)
+                    lines = raw1[(name, o)][:].rearrange("p j (b u s i e) -> p u b s j i e", u=2, s=4, i=2, e=2)[:, u]
+                    nc.vector.tensor_copy(out=g[:].rearrange("p e b (s i) j -> p b s j i e", i=2), in_=lines)
                 grouped.append(g)
             slots = []
             for u in range(2):

@@ -19,12 +19,12 @@ P = 128
 PACK = 4
 PASSES = K // (P * PACK)
 BLOCK = 128
-H_CHUNK = 1024
-LAG = 3
-SCALAR_SECOND = {"w2"}
-OUT_CHUNKS = [256,256,256,256]
-SCALAR_CASTS = {("w1", 1, 1)}
-VECTOR_RELUS = {("r1", 2), ("r1", 5)}
+CHUNK = 256
+SCALAR_SECOND = set()
+OUT_CHUNKS = [256, 256, 256, 128, 128]
+SCALAR_CASTS = {("w1", 1, 0), ("w1", 1, 1), ("w1", 0, 1)}
+VECTOR_RELUS = {("r1", 6)}
+LATE_BLOCKS = 2
 
 
 def tile_picked_yrnd_norm_p_kernel(
@@ -113,14 +113,12 @@ def tile_picked_yrnd_norm_p_kernel(
             grouped = []
             for u in range(2):
                 g = tile([P, 2, 16, 8, PACK], BF16, "g_%s_%d_%d" % (name, o, u))
-                src = raw1[(name, o)][:].rearrange("p j (b u q e) -> p u b q e j", u=2, q=8, e=2)[:, u]
-                dst = g[:].rearrange("p e b q j -> p b q e j")
+                src = raw1[(name, o)][:].rearrange("p j (b u s i e) -> p u b s j i e", u=2, s=4, i=2, e=2)[:, u]
+                dst = g[:].rearrange("p e b (s i) j -> p b s j i e", i=2)
                 if (name, o, u) in SCALAR_CASTS:
-                    for e in range(2):
-                        nc.scalar.activation(out=dst[:, :, :, e, :], in_=src[:, :, :, e, :], func=ACT.Copy)
+                    nc.scalar.copy(out=dst, in_=src)
                 else:
-                    lines = raw1[(name, o)][:].rearrange("p j (b u s i e) -> p u b s j i e", u=2, s=4, i=2, e=2)[:, u]
-                    nc.vector.tensor_copy(out=g[:].rearrange("p e b (s i) j -> p b s j i e", i=2), in_=lines)
+                    nc.vector.tensor_copy(out=dst, in_=src)
                 grouped.append(g)
             slots = []
             for u in range(2):
@@ -131,7 +129,7 @@ def tile_picked_yrnd_norm_p_kernel(
                     slots.append((codes[:, e * P : (e + 1) * P], plane[:, e * P : (e + 1) * P]))
             return slots
 
-        def second_weights(name, sign):
+        def cast_second(name, sign):
             g = tile([P, N, PACK], BF16, "g_%s" % name)
             src = raw2[name][:].rearrange("p t (c i) -> p c t i", i=4)
             dst = g[:].rearrange("p (c i) t -> p c t i", i=4)
@@ -139,50 +137,65 @@ def tile_picked_yrnd_norm_p_kernel(
                 nc.scalar.activation(out=dst, in_=src, func=ACT.Copy, scale=sign)
             else:
                 nc.vector.tensor_scalar(out=dst, in0=src, scalar1=sign, scalar2=None, op0=ALU.mult)
-            return quantize(g[:].rearrange("p n t -> p (n t)"), N, "q_%s" % name)
+            return g[:].rearrange("p n t -> p (n t)")
 
-        def hidden_pass(acc, slots, o, block):
+        def hidden_block(name, weights, block, dst):
+            acc = psum.tile([P, 512], F32, name="bank")
             half, col = divmod(block * BLOCK, 512)
-            for t in range(PACK):
-                codes, plane = slots[t]
-                nc.tensor.matmul_mx(
-                    out=acc[:, t * BLOCK : (t + 1) * BLOCK],
-                    lhsT=codes.bitcast(FP8X4),
-                    lhsT_scale=plane,
-                    rhs=x_codes[(o, half)][:, col : col + BLOCK].bitcast(FP8X4),
-                    rhs_scale=x_planes[o][:, block * BLOCK : (block + 1) * BLOCK],
-                    start=(o == 0 and t == 0),
-                    stop=(o == PASSES - 1 and t == PACK - 1),
-                )
+            late = name == "r1" and block >= S // BLOCK - LATE_BLOCKS
+            for i, o in enumerate((1, 0) if late else (0, 1)):
+                for t in range(PACK):
+                    codes, plane = weights[o][t]
+                    nc.tensor.matmul_mx(
+                        out=acc[:, t * BLOCK : (t + 1) * BLOCK],
+                        lhsT=codes.bitcast(FP8X4),
+                        lhsT_scale=plane,
+                        rhs=x_codes[(o, half)][:, col : col + BLOCK].bitcast(FP8X4),
+                        rhs_scale=x_planes[o][:, block * BLOCK : (block + 1) * BLOCK],
+                        start=(i == 0 and t == 0),
+                        stop=(i == PASSES - 1 and t == PACK - 1),
+                    )
+            src = acc[:].rearrange("p (t n) -> p n t", t=PACK)
+            if (name, block) in VECTOR_RELUS:
+                nc.vector.tensor_scalar(out=dst, in0=src, scalar1=0.0, scalar2=None, op0=ALU.max)
+            else:
+                nc.scalar.activation(out=dst, in_=src, func=ACT.Relu)
 
-        def hidden_chunk(name, weights, start, width, tag=None):
+        def hidden_chunk(name, weights, start, width):
             grouped = tile([P, width, PACK], BF16, "hid_%s_%d" % (name, start))
             for n0 in range(0, width, BLOCK):
-                block = (start + n0) // BLOCK
-                acc = psum.tile([P, 512], F32, name="bank")
-                for o in range(PASSES):
-                    hidden_pass(acc, weights[o], o, block)
-                src = acc[:].rearrange("p (t n) -> p n t", t=PACK)
-                dst = grouped[:, n0 : n0 + BLOCK, :]
-                if (name, block) in VECTOR_RELUS:
-                    nc.vector.tensor_scalar(out=dst, in0=src, scalar1=0.0, scalar2=None, op0=ALU.max)
-                else:
-                    nc.scalar.activation(out=dst, in_=src, func=ACT.Relu)
-            return quantize(grouped[:].rearrange("p n t -> p (n t)"), width, "q_hid_%s_%d" % (name, start), tag)
+                hidden_block(name, weights, (start + n0) // BLOCK, grouped[:, n0 : n0 + BLOCK, :])
+            return grouped[:].rearrange("p n t -> p (n t)")
+
+        def quantize_into(mx, col, grouped):
+            cols = slice(col, col + grouped.shape[1] // PACK)
+            nc.vector.quantize_mx(out=mx[0][:, cols].bitcast(FP8X4), scales=mx[1][:, cols], in_=grouped)
 
         w1_q = [first_weights("w1", o) for o in range(PASSES)]
         r1_q = [first_weights("r1", o) for o in range(PASSES)]
-        h_q = [hidden_chunk("w1", w1_q, start, H_CHUNK, "raw_r1_1") for start in range(0, S, H_CHUNK)]
-        w2_q = second_weights("w2", 1.0)
-        r2_q = second_weights("r2", -1.0)
+        h_hid = [hidden_chunk("w1", w1_q, start, CHUNK) for start in range(0, S, CHUNK)]
+        g_w2 = cast_second("w2", 1.0)
+        h_codes = tile([P, S], U32, "h_codes")
+        h_planes = [tile([P, CHUNK], U8, "h_plane_early", "g_r1_0_0"), tile([P, S], U8, "h_plane_late", "g_r1_1_0")]
+        quantize_into((h_codes, h_planes[0]), 0, h_hid[0])
+        quantize_into((h_codes, h_planes[1]), CHUNK, h_hid[1])
+        g_r2 = cast_second("r2", -1.0)
+        quantize_into((h_codes, h_planes[1]), 2 * CHUNK, h_hid[2])
+        quantize_into((h_codes, h_planes[1]), 3 * CHUNK, h_hid[3])
+        w2_q = quantize(g_w2, N, "q_w2")
+        r2_q = quantize(g_r2, N, "q_r2")
 
+        starts = [sum(OUT_CHUNKS[:i]) for i in range(len(OUT_CHUNKS))]
 
-        def output_chunk(start, width, g_codes, g_plane):
-            h_codes, h_plane = h_q[start // H_CHUNK]
-            h_cols = slice(start % H_CHUNK, start % H_CHUNK + width)
+        def hidden_codes(i):
+            return quantize(hidden_chunk("r1", r1_q, starts[i], OUT_CHUNKS[i]), OUT_CHUNKS[i], "q_g%d" % i)
+
+        def output_chunk(i, g_mx):
+            start, width = starts[i], OUT_CHUNKS[i]
+            states = slice(start, start + width)
+            products = ((w2_q, h_codes[:, states], h_planes[min(i, 1)][:, states]), (r2_q, g_mx[0][:], g_mx[1][:]))
             acc = psum.tile([P, 512], F32, name="bank")
-            products = ((w2_q, h_codes[:, h_cols], h_plane[:, h_cols]), (r2_q, g_codes[:], g_plane[:]))
-            for i, (weights, codes, plane) in enumerate(products):
+            for j, (weights, codes, plane) in enumerate(products):
                 for m in range(2):
                     rows = slice(m * P, (m + 1) * P)
                     nc.tensor.matmul_mx(
@@ -191,24 +204,28 @@ def tile_picked_yrnd_norm_p_kernel(
                         lhsT_scale=weights[1][:, rows],
                         rhs=codes.bitcast(FP8X4),
                         rhs_scale=plane,
-                        start=(i == 0 and m == 0),
-                        stop=(i == 1 and m == 1),
+                        start=(j == 0 and m == 0),
+                        stop=(j == 1 and m == 1),
                     )
+            squared = tile([P, 2, width], F32, "squared%d" % i)
             for m in range(2):
-                squared = tile([P, width], F32, "squared%d_%d" % (start, m))
                 nc.scalar.activation(
-                    out=squared[:], in_=acc[:, m * width : (m + 1) * width], func=ACT.Square, scale=inv_sb[:, m : m + 1]
+                    out=squared[:, m, :],
+                    in_=acc[:, m * width : (m + 1) * width],
+                    func=ACT.Square,
+                    scale=inv_sb[:, m : m + 1],
                 )
-                result = tile([P, width], F32, "result%d_%d" % (start, m))
+            result = tile([P, 2, width], F32, "result%d" % i)
+            parts = [slice(0, 1), slice(1, 2)] if width > BLOCK else [slice(0, 2)]
+            for part in parts:
                 nc.vector.tensor_tensor(
-                    out=result[:], in0=squared[:], in1=cap_sb[:, m, start : start + width], op=ALU.min
+                    out=result[:, part, :], in0=squared[:, part, :], in1=cap_sb[:, part, states], op=ALU.min
                 )
-                nc.sync.dma_start(out=out[m * P : (m + 1) * P, start : start + width], in_=result[:])
+                nc.sync.dma_start(out=out.rearrange("(m p) j -> p m j", p=P)[:, part, states], in_=result[:, part, :])
 
-        starts = [sum(OUT_CHUNKS[:i]) for i in range(len(OUT_CHUNKS))]
-        g_q = []
-        for i in range(len(OUT_CHUNKS) + LAG):
-            if i < len(OUT_CHUNKS):
-                g_q.append(hidden_chunk("r1", r1_q, starts[i], OUT_CHUNKS[i]))
-            if i >= LAG:
-                output_chunk(starts[i - LAG], OUT_CHUNKS[i - LAG], *g_q[i - LAG])
+        last = len(OUT_CHUNKS) - 1
+        g_q = [hidden_codes(i) for i in range(last)]
+        output_chunk(0, g_q[0])
+        g_q.append(hidden_codes(last))
+        for i in range(1, last + 1):
+            output_chunk(i, g_q[i])

@@ -22,7 +22,7 @@ BLOCK = 128
 CHUNK = 256
 SCALAR_SECOND = set()
 OUT_CHUNKS = [256, 256, 256, 128, 128]
-SCALAR_CASTS = {("w1", 1, 0), ("w1", 1, 1), ("w1", 0, 1)}
+SCALAR_CASTS = {("w1", 1, 1)}
 VECTOR_RELUS = {("r1", 6)}
 LATE_BLOCKS = 2
 
@@ -113,12 +113,14 @@ def tile_picked_yrnd_norm_p_kernel(
             grouped = []
             for u in range(2):
                 g = tile([P, 2, 16, 8, PACK], BF16, "g_%s_%d_%d" % (name, o, u))
-                src = raw1[(name, o)][:].rearrange("p j (b u s i e) -> p u b s j i e", u=2, s=4, i=2, e=2)[:, u]
-                dst = g[:].rearrange("p e b (s i) j -> p b s j i e", i=2)
+                src = raw1[(name, o)][:].rearrange("p j (b u q e) -> p u b q e j", u=2, q=8, e=2)[:, u]
+                dst = g[:].rearrange("p e b q j -> p b q e j")
                 if (name, o, u) in SCALAR_CASTS:
-                    nc.scalar.copy(out=dst, in_=src)
+                    for e in range(2):
+                        nc.scalar.activation(out=dst[:, :, :, e, :], in_=src[:, :, :, e, :], func=ACT.Copy)
                 else:
-                    nc.vector.tensor_copy(out=dst, in_=src)
+                    lines = raw1[(name, o)][:].rearrange("p j (b u s i e) -> p u b s j i e", u=2, s=4, i=2, e=2)[:, u]
+                    nc.vector.tensor_copy(out=g[:].rearrange("p e b (s i) j -> p b s j i e", i=2), in_=lines)
                 grouped.append(g)
             slots = []
             for u in range(2):

@@ -91,8 +91,13 @@ def tile_picked_yrnd_norm_p_kernel(
         inv_sb = tile([P, 2], F32, "inv_sb")
         with nc.allow_non_contiguous_dma(reason="one factor for each output row"):
             nc.sync.dma_start(out=inv_sb[:], in_=inv.rearrange("(m p) u -> p (m u)", p=P))
-        cap_sb = tile([P, 2, S], F32, "cap_sb")
-        nc.sync.dma_start(out=cap_sb[:], in_=capv.rearrange("(m p) j -> p m j", p=P))
+        cap_halves = []
+        for a in range(2):
+            cap_sb = tile([P, 2, S // 2], F32, "cap_sb%d" % a)
+            nc.sync.dma_start(
+                out=cap_sb[:], in_=capv.rearrange("(m p) j -> p m j", p=P)[:, :, a * (S // 2) : (a + 1) * (S // 2)]
+            )
+            cap_halves.append(cap_sb)
 
         x_codes = {}
         for o in range(PASSES):
@@ -218,10 +223,12 @@ def tile_picked_yrnd_norm_p_kernel(
                     scale=inv_sb[:, m : m + 1],
                 )
             result = tile([P, 2, width], F32, "result%d" % i)
+            a, c0 = divmod(start, S // 2)
+            cap = cap_halves[a][:, :, c0 : c0 + width]
             parts = [slice(0, 1), slice(1, 2)] if width > BLOCK else [slice(0, 2)]
             for part in parts:
                 nc.vector.tensor_tensor(
-                    out=result[:, part, :], in0=squared[:, part, :], in1=cap_sb[:, part, states], op=ALU.min
+                    out=result[:, part, :], in0=squared[:, part, :], in1=cap[:, part, :], op=ALU.min
                 )
                 nc.sync.dma_start(out=out.rearrange("(m p) j -> p m j", p=P)[:, part, states], in_=result[:, part, :])
 

@@ -1,6 +1,7 @@
 from contextlib import ExitStack
 
 import concourse.mybir as mybir
+from concourse.masks import make_identity
 
 K, T, S, H, N = 1024, 4096, 1024, 512, 256
 FLOPS = 2 * S * (2 * K * H + 2 * H * N)
@@ -72,6 +73,15 @@ def tile_picked_yrnd_norm_p_kernel(
             out=scale_table[0:P:4, :].bitcast(I32),
             in_=x_scales.rearrange("o q c -> (o q) c").bitcast(I32),
         )
+        inv_rows = tile([P, P], F32, "inv_rows")
+        nc.gpsimd.memset(inv_rows[:], 0.0)
+        nc.sync.dma_start(out=inv_rows[0:2, :], in_=inv.rearrange("(m p) u -> m (p u)", p=P))
+        identity = tile([P, P], F32, "identity")
+        make_identity(nc, identity[:])
+        turned = psum.tile([P, 512], F32, name="bank")
+        nc.tensor.transpose(turned[:, 0:P], inv_rows[:], identity[:])
+        inv_sb = tile([P, 2], F32, "inv_sb")
+        nc.scalar.copy(out=inv_sb[:], in_=turned[:, 0:2])
         load_words(0)
         load_first("w1", w1, 0)
         picked_scales = tile([P, S], U8, "picked_scales")
@@ -84,13 +94,8 @@ def tile_picked_yrnd_norm_p_kernel(
         raw2 = {}
         for name, w in (("w2", w2), ("r2", r2)):
             raw = tile([P, PACK, N], F32, "raw_%s" % name)
-            rows = w.rearrange("(b u q e) n -> u b q (e n)", u=2, q=8, e=2)
-            for u in range(2):
-                nc.sync.dma_start(out=raw[:, 2 * u : 2 * u + 2, :].rearrange("p e n -> p (e n)"), in_=rows[u])
+            nc.sync.dma_start(out=raw[:], in_=w.rearrange("(p j) n -> p j n", j=PACK))
             raw2[name] = raw
-        inv_sb = tile([P, 2], F32, "inv_sb")
-        with nc.allow_non_contiguous_dma(reason="one factor for each output row"):
-            nc.sync.dma_start(out=inv_sb[:], in_=inv.rearrange("(m p) u -> p (m u)", p=P))
         cap_halves = []
         for a in range(2):
             cap_sb = tile([P, 2, S // 2], F32, "cap_sb%d" % a)
@@ -114,23 +119,22 @@ def tile_picked_yrnd_norm_p_kernel(
             nc.vector.quantize_mx(out=codes[:].bitcast(FP8X4), scales=plane[:], in_=grouped)
             return codes, plane
 
-        def first_weights(name, o):
+        def first_weights(name, o, tag=None):
             grouped = []
             for u in range(2):
-                g = tile([P, 2, 16, 8, PACK], BF16, "g_%s_%d_%d" % (name, o, u))
-                src = raw1[(name, o)][:].rearrange("p j (b u q e) -> p u b q e j", u=2, q=8, e=2)[:, u]
-                dst = g[:].rearrange("p e b q j -> p b q e j")
+                g = tile([P, 2, P, PACK], BF16, "g_%s_%d_%d" % (name, o, u), tag if u == 0 else None)
+                src = raw1[(name, o)][:].rearrange("p j (m u e) -> p u m j e", u=2, e=2)[:, u]
+                dst = g[:].rearrange("p e m j -> p m j e")
                 if (name, o, u) in SCALAR_CASTS:
                     for e in range(2):
-                        nc.scalar.activation(out=dst[:, :, :, e, :], in_=src[:, :, :, e, :], func=ACT.Copy)
+                        nc.scalar.activation(out=dst[:, :, :, e], in_=src[:, :, :, e], func=ACT.Copy)
                 else:
-                    lines = raw1[(name, o)][:].rearrange("p j (b u s i e) -> p u b s j i e", u=2, s=4, i=2, e=2)[:, u]
-                    nc.vector.tensor_copy(out=g[:].rearrange("p e b (s i) j -> p b s j i e", i=2), in_=lines)
+                    nc.vector.tensor_copy(out=dst, in_=src)
                 grouped.append(g)
             slots = []
             for u in range(2):
                 codes, plane = quantize(
-                    grouped[u][:].rearrange("p e b q j -> p (e b q j)"), 2 * P, "q_%s_%d_%d" % (name, o, u)
+                    grouped[u][:].rearrange("p e m j -> p (e m j)"), 2 * P, "q_%s_%d_%d" % (name, o, u)
                 )
                 for e in range(2):
                     slots.append((codes[:, e * P : (e + 1) * P], plane[:, e * P : (e + 1) * P]))
@@ -178,7 +182,7 @@ def tile_picked_yrnd_norm_p_kernel(
             cols = slice(col, col + grouped.shape[1] // PACK)
             nc.vector.quantize_mx(out=mx[0][:, cols].bitcast(FP8X4), scales=mx[1][:, cols], in_=grouped)
 
-        w1_q = [first_weights("w1", o) for o in range(PASSES)]
+        w1_q = [first_weights("w1", 0), first_weights("w1", 1, "scale_table")]
         r1_q = [first_weights("r1", o) for o in range(PASSES)]
         h_hid = [hidden_chunk("w1", w1_q, start, CHUNK) for start in range(0, S, CHUNK)]
         g_w2 = cast_second("w2", 1.0)

@@ -21,10 +21,10 @@ PACK = 4
 PASSES = K // (P * PACK)
 BLOCK = 128
 CHUNK = 256
-SCALAR_SECOND = set()
+SCALAR_SECOND = {"w2"}
 OUT_CHUNKS = [256, 256, 256, 128, 128]
 SCALAR_CASTS = {("w1", 1, 1)}
-VECTOR_RELUS = {("r1", 6)}
+VECTOR_RELUS = {("r1", 4), ("r1", 6)}
 LATE_BLOCKS = 2
 
 

@@ -25,7 +25,7 @@ SCALAR_SECOND = {"w2"}
 OUT_CHUNKS = [256, 256, 256, 128, 128]
 SCALAR_CASTS = {("w1", 1, 1)}
 VECTOR_RELUS = {("r1", 4), ("r1", 6)}
-LATE_BLOCKS = 2
+LATE_BLOCKS = 0
 
 
 def tile_picked_yrnd_norm_p_kernel(

@@ -21,11 +21,10 @@ PACK = 4
 PASSES = K // (P * PACK)
 BLOCK = 128
 CHUNK = 256
-SCALAR_SECOND = {"w2"}
+GATHERS = ([512, 512], [256, 256, 512])
 OUT_CHUNKS = [256, 256, 256, 128, 128]
-SCALAR_CASTS = {("w1", 1, 1)}
-VECTOR_RELUS = {("r1", 4), ("r1", 6)}
-LATE_BLOCKS = 0
+EARLY_H = 1
+OUT_BANKS = [0, 1, 2, 3, 4]
 
 
 def tile_picked_yrnd_norm_p_kernel(
@@ -34,32 +33,24 @@ def tile_picked_yrnd_norm_p_kernel(
     nc = tc.nc
     with ExitStack() as ctx:
         keep = ctx.enter_context(tc.tile_pool(name="keep", bufs=1))
-        psum = ctx.enter_context(tc.psum_pool(name="psum", bufs=8))
+        psum = ctx.enter_context(tc.psum_pool(name="psum", bufs=1))
 
         def tile(shape, dtype, name, tag=None):
             return keep.tile(shape, dtype, name=name, tag=tag or name, align_bytes=64)
 
-        offsets = keep.tile([P, S // 16], U16, name="offsets")
-        nc.sync.dma_start(offsets[:], offs)
+        def bank(index, name):
+            return psum.tile([P, 512], F32, name=name, tag="bank%d" % index)
 
-        scale_table = tile([P, T], U8, "scale_table")
-        nc.vector.memset(scale_table[:].bitcast(I32), 0)
-        x_planes = [tile([P, S], U8, "x_plane%d" % o) for o in range(PASSES)]
-        for plane in x_planes:
-            nc.vector.memset(plane[:].bitcast(I32), 0)
-
-        raw1 = {}
-        word_tables = []
-
-        def load_first(name, w, o):
-            raw = tile([P, PACK, H], F32, "raw_%s_%d" % (name, o))
-            nc.sync.dma_start(out=raw[:], in_=w[o * 512 : (o + 1) * 512, :].rearrange("(p j) c -> p j c", j=PACK))
-            raw1[(name, o)] = raw
+        def load_rows(w, first_row, width, name):
+            raw = tile([P, PACK, width], F32, name)
+            rows = w[first_row : first_row + P * PACK, :]
+            nc.sync.dma_start(out=raw[:], in_=rows.rearrange("(p j) c -> p j c", j=PACK))
+            return raw
 
         def load_words(o):
             table = tile([P, T], I32, "word_table%d" % o)
             nc.sync.dma_start(out=table[:], in_=x_words[o].rearrange("p c r -> p (c r)").bitcast(I32))
-            word_tables.append(table)
+            return table
 
         def move_scales(o):
             for r in range(4):
@@ -68,34 +59,37 @@ def tile_picked_yrnd_norm_p_kernel(
                     in_=picked_scales[64 * o + 4 * r : 64 * o + 64 : 16, :].bitcast(I32),
                 )
 
-        load_first("w1", w1, 1)
-        nc.sync.dma_start(
-            out=scale_table[0:P:4, :].bitcast(I32),
-            in_=x_scales.rearrange("o q c -> (o q) c").bitcast(I32),
-        )
+        offsets = keep.tile([P, S // 16], U16, name="offsets")
+        scale_table = tile([P, T], U8, "scale_table")
+        nc.vector.memset(scale_table[:].bitcast(I32), 0)
+        x_planes = [tile([P, S], U8, "x_plane%d" % o) for o in range(PASSES)]
+        for plane in x_planes:
+            nc.vector.memset(plane[:].bitcast(I32), 0)
         inv_rows = tile([P, P], F32, "inv_rows")
         nc.gpsimd.memset(inv_rows[:], 0.0)
-        nc.sync.dma_start(out=inv_rows[0:2, :], in_=inv.rearrange("(m p) u -> m (p u)", p=P))
         identity = tile([P, P], F32, "identity")
         make_identity(nc, identity[:])
-        turned = psum.tile([P, 512], F32, name="bank")
+
+        nc.sync.dma_start(offsets[:], offs)
+        w1_raw = [None, load_rows(w1, 512, H, "w1_raw1")]
+        nc.sync.dma_start(
+            out=scale_table[0:P:4, :].bitcast(I32), in_=x_scales.rearrange("o q c -> (o q) c").bitcast(I32)
+        )
+        nc.sync.dma_start(out=inv_rows[0:2, :], in_=inv.rearrange("(m p) u -> m (p u)", p=P))
+        turned = bank(7, "turned")
         nc.tensor.transpose(turned[:, 0:P], inv_rows[:], identity[:])
         inv_sb = tile([P, 2], F32, "inv_sb")
         nc.scalar.copy(out=inv_sb[:], in_=turned[:, 0:2])
-        load_words(0)
-        load_first("w1", w1, 0)
+        word_tables = [load_words(0)]
+        w1_raw[0] = load_rows(w1, 0, H, "w1_raw0")
         picked_scales = tile([P, S], U8, "picked_scales")
         nc.vector.tensor_copy(out=picked_scales[:], in_=scale_table[:].indirect(offsets[:]))
         move_scales(0)
-        load_words(1)
+        word_tables.append(load_words(1))
         move_scales(1)
-        load_first("r1", r1, 0)
-        load_first("r1", r1, 1)
-        raw2 = {}
-        for name, w in (("w2", w2), ("r2", r2)):
-            raw = tile([P, PACK, N], F32, "raw_%s" % name)
-            nc.sync.dma_start(out=raw[:], in_=w.rearrange("(p j) n -> p j n", j=PACK))
-            raw2[name] = raw
+        r1_raw = [load_rows(r1, 512 * o, H, "r1_raw%d" % o) for o in range(PASSES)]
+        w2_raw = load_rows(w2, 0, N, "w2_raw")
+        r2_raw = load_rows(r2, 0, N, "r2_raw")
         cap_halves = []
         for a in range(2):
             cap_sb = tile([P, 2, S // 2], F32, "cap_sb%d" % a)
@@ -104,28 +98,30 @@ def tile_picked_yrnd_norm_p_kernel(
             )
             cap_halves.append(cap_sb)
 
-        x_codes = {}
+        x_codes = [[], []]
         for o in range(PASSES):
-            for half in range(2):
-                codes = tile([P, 512], U32, "x_codes%d_%d" % (o, half))
-                nc.vector.tensor_copy(
-                    out=codes[:], in_=word_tables[o][:].bitcast(U32).indirect(offsets[:, 32 * half : 32 * half + 32])
-                )
-                x_codes[(o, half)] = codes
+            start = 0
+            for width in GATHERS[o]:
+                codes = tile([P, width], U32, "x_codes%d_%d" % (o, start))
+                picks = offsets[:, start // 16 : (start + width) // 16]
+                nc.vector.tensor_copy(out=codes[:], in_=word_tables[o][:].bitcast(U32).indirect(picks))
+                x_codes[o].extend(codes[:, c : c + BLOCK] for c in range(0, width, BLOCK))
+                start = start + width
 
-        def quantize(grouped, width, name, tag=None):
-            codes = tile([P, width], U32, name + "_codes", tag)
+        def quantize(grouped, name):
+            width = grouped.shape[1] // PACK
+            codes = tile([P, width], U32, name + "_codes")
             plane = tile([P, width], U8, name + "_plane")
             nc.vector.quantize_mx(out=codes[:].bitcast(FP8X4), scales=plane[:], in_=grouped)
             return codes, plane
 
-        def first_weights(name, o, tag=None):
+        def first_weights(raw, name, tag=None, scalar_second=False):
             grouped = []
             for u in range(2):
-                g = tile([P, 2, P, PACK], BF16, "g_%s_%d_%d" % (name, o, u), tag if u == 0 else None)
-                src = raw1[(name, o)][:].rearrange("p j (m u e) -> p u m j e", u=2, e=2)[:, u]
+                g = tile([P, 2, P, PACK], BF16, "%s_g%d" % (name, u), tag if u == 0 else None)
+                src = raw[:].rearrange("p j (m u e) -> p u m j e", u=2, e=2)[:, u]
                 dst = g[:].rearrange("p e m j -> p m j e")
-                if (name, o, u) in SCALAR_CASTS:
+                if scalar_second and u == 1:
                     for e in range(2):
                         nc.scalar.activation(out=dst[:, :, :, e], in_=src[:, :, :, e], func=ACT.Copy)
                 else:
@@ -133,79 +129,92 @@ def tile_picked_yrnd_norm_p_kernel(
                 grouped.append(g)
             slots = []
             for u in range(2):
-                codes, plane = quantize(
-                    grouped[u][:].rearrange("p e m j -> p (e m j)"), 2 * P, "q_%s_%d_%d" % (name, o, u)
-                )
-                for e in range(2):
-                    slots.append((codes[:, e * P : (e + 1) * P], plane[:, e * P : (e + 1) * P]))
+                codes, plane = quantize(grouped[u][:].rearrange("p e m j -> p (e m j)"), "%s_q%d" % (name, u))
+                slots.extend((codes[:, e * P : (e + 1) * P], plane[:, e * P : (e + 1) * P]) for e in range(2))
             return slots
 
-        def cast_second(name, sign):
-            g = tile([P, N, PACK], BF16, "g_%s" % name)
-            src = raw2[name][:].rearrange("p t (c i) -> p c t i", i=4)
+        def second_views(raw, name):
+            g = tile([P, N, PACK], BF16, name)
+            src = raw[:].rearrange("p t (c i) -> p c t i", i=4)
             dst = g[:].rearrange("p (c i) t -> p c t i", i=4)
-            if name in SCALAR_SECOND:
-                nc.scalar.activation(out=dst, in_=src, func=ACT.Copy, scale=sign)
-            else:
-                nc.vector.tensor_scalar(out=dst, in0=src, scalar1=sign, scalar2=None, op0=ALU.mult)
-            return g[:].rearrange("p n t -> p (n t)")
+            return src, dst, g[:].rearrange("p n t -> p (n t)")
 
-        def hidden_block(name, weights, block, dst):
-            acc = psum.tile([P, 512], F32, name="bank")
-            half, col = divmod(block * BLOCK, 512)
-            late = name == "r1" and block >= S // BLOCK - LATE_BLOCKS
-            for i, o in enumerate((1, 0) if late else (0, 1)):
+        def first_layer(weights, block, acc):
+            for o in range(PASSES):
                 for t in range(PACK):
                     codes, plane = weights[o][t]
                     nc.tensor.matmul_mx(
                         out=acc[:, t * BLOCK : (t + 1) * BLOCK],
                         lhsT=codes.bitcast(FP8X4),
                         lhsT_scale=plane,
-                        rhs=x_codes[(o, half)][:, col : col + BLOCK].bitcast(FP8X4),
+                        rhs=x_codes[o][block].bitcast(FP8X4),
                         rhs_scale=x_planes[o][:, block * BLOCK : (block + 1) * BLOCK],
-                        start=(i == 0 and t == 0),
-                        stop=(i == PASSES - 1 and t == PACK - 1),
+                        start=(o == 0 and t == 0),
+                        stop=(o == PASSES - 1 and t == PACK - 1),
                     )
-            src = acc[:].rearrange("p (t n) -> p n t", t=PACK)
-            if (name, block) in VECTOR_RELUS:
-                nc.vector.tensor_scalar(out=dst, in0=src, scalar1=0.0, scalar2=None, op0=ALU.max)
-            else:
-                nc.scalar.activation(out=dst, in_=src, func=ACT.Relu)
+            return acc[:].rearrange("p (t n) -> p n t", t=PACK)
 
-        def hidden_chunk(name, weights, start, width):
-            grouped = tile([P, width, PACK], BF16, "hid_%s_%d" % (name, start))
-            for n0 in range(0, width, BLOCK):
-                hidden_block(name, weights, (start + n0) // BLOCK, grouped[:, n0 : n0 + BLOCK, :])
-            return grouped[:].rearrange("p n t -> p (n t)")
+        def relu_scalar(dst, src):
+            nc.scalar.activation(out=dst, in_=src, func=ACT.Relu)
 
-        def quantize_into(mx, col, grouped):
-            cols = slice(col, col + grouped.shape[1] // PACK)
-            nc.vector.quantize_mx(out=mx[0][:, cols].bitcast(FP8X4), scales=mx[1][:, cols], in_=grouped)
+        def relu_vector(dst, src):
+            nc.vector.tensor_scalar(out=dst, in0=src, scalar1=0.0, scalar2=None, op0=ALU.max)
 
-        w1_q = [first_weights("w1", 0), first_weights("w1", 1, "scale_table")]
-        r1_q = [first_weights("r1", o) for o in range(PASSES)]
-        h_hid = [hidden_chunk("w1", w1_q, start, CHUNK) for start in range(0, S, CHUNK)]
-        g_w2 = cast_second("w2", 1.0)
+        w1_q = [first_weights(w1_raw[0], "w1_0"), first_weights(w1_raw[1], "w1_1", "scale_table", True)]
+        h_hid = []
+        for c in range(S // CHUNK):
+            grouped = tile([P, CHUNK, PACK], BF16, "h_hid%d" % c)
+            for n0 in range(0, CHUNK, BLOCK):
+                block = (c * CHUNK + n0) // BLOCK
+                relu_scalar(grouped[:, n0 : n0 + BLOCK, :], first_layer(w1_q, block, bank(block, "h_acc%d" % block)))
+            h_hid.append(grouped[:].rearrange("p n t -> p (n t)"))
+
         h_codes = tile([P, S], U32, "h_codes")
-        h_planes = [tile([P, CHUNK], U8, "h_plane_early", "g_r1_0_0"), tile([P, S], U8, "h_plane_late", "g_r1_1_0")]
-        quantize_into((h_codes, h_planes[0]), 0, h_hid[0])
-        quantize_into((h_codes, h_planes[1]), CHUNK, h_hid[1])
-        g_r2 = cast_second("r2", -1.0)
-        quantize_into((h_codes, h_planes[1]), 2 * CHUNK, h_hid[2])
-        quantize_into((h_codes, h_planes[1]), 3 * CHUNK, h_hid[3])
-        w2_q = quantize(g_w2, N, "q_w2")
-        r2_q = quantize(g_r2, N, "q_r2")
+        h_planes = []
+
+        def quantize_h(c):
+            cols = slice(c * CHUNK, (c + 1) * CHUNK)
+            nc.vector.quantize_mx(out=h_codes[:, cols].bitcast(FP8X4), scales=h_planes[-1][:, cols], in_=h_hid[c])
+
+        r1_q = [first_weights(r1_raw[0], "r1_0")]
+        h_planes.append(tile([P, S], U8, "h_plane_early", "r1_0_g0"))
+        for c in range(EARLY_H):
+            quantize_h(c)
+        r1_q.append(first_weights(r1_raw[1], "r1_1"))
+        h_planes.append(tile([P, S], U8, "h_plane_late", "r1_1_g0"))
+        for c in range(EARLY_H, S // CHUNK):
+            quantize_h(c)
+
+        src, dst, w2_grouped = second_views(w2_raw, "w2_g")
+        nc.scalar.activation(out=dst, in_=src, func=ACT.Copy)
+        src, dst, r2_grouped = second_views(r2_raw, "r2_g")
+        nc.vector.tensor_scalar(out=dst, in0=src, scalar1=-1.0, scalar2=None, op0=ALU.mult)
+        w2_q = quantize(w2_grouped, "w2_q")
+        r2_q = quantize(r2_grouped, "r2_q")
 
         starts = [sum(OUT_CHUNKS[:i]) for i in range(len(OUT_CHUNKS))]
+        g_hid = {}
+        g_q = {}
+        squared = {}
 
-        def hidden_codes(i):
-            return quantize(hidden_chunk("r1", r1_q, starts[i], OUT_CHUNKS[i]), OUT_CHUNKS[i], "q_g%d" % i)
+        def g_chunk(i, relu, tag=None):
+            g_hid[i] = tile([P, OUT_CHUNKS[i], PACK], BF16, "g_hid%d" % i, tag)
+            for n0 in range(0, OUT_CHUNKS[i], BLOCK):
+                g_block(i, n0, relu)
 
-        def output_chunk(i, g_mx):
-            start, width = starts[i], OUT_CHUNKS[i]
-            states = slice(start, start + width)
-            products = ((w2_q, h_codes[:, states], h_planes[min(i, 1)][:, states]), (r2_q, g_mx[0][:], g_mx[1][:]))
-            acc = psum.tile([P, 512], F32, name="bank")
+        def g_block(i, n0, relu):
+            block = (starts[i] + n0) // BLOCK
+            relu(g_hid[i][:, n0 : n0 + BLOCK, :], first_layer(r1_q, block, bank(block, "g_acc%d" % block)))
+
+        def quantize_g(i):
+            g_q[i] = quantize(g_hid[i][:].rearrange("p n t -> p (n t)"), "g_q%d" % i)
+
+        def square_chunk(i):
+            width = OUT_CHUNKS[i]
+            states = slice(starts[i], starts[i] + width)
+            h_plane = h_planes[0 if starts[i] < EARLY_H * CHUNK else 1]
+            products = ((w2_q, h_codes[:, states], h_plane[:, states]), (r2_q, g_q[i][0][:], g_q[i][1][:]))
+            acc = bank(OUT_BANKS[i], "out_acc%d" % i)
             for j, (weights, codes, plane) in enumerate(products):
                 for m in range(2):
                     rows = slice(m * P, (m + 1) * P)
@@ -218,27 +227,41 @@ def tile_picked_yrnd_norm_p_kernel(
                         start=(j == 0 and m == 0),
                         stop=(j == 1 and m == 1),
                     )
-            squared = tile([P, 2, width], F32, "squared%d" % i)
+            squared[i] = tile([P, 2, width], F32, "squared%d" % i)
             for m in range(2):
                 nc.scalar.activation(
-                    out=squared[:, m, :],
+                    out=squared[i][:, m, :],
                     in_=acc[:, m * width : (m + 1) * width],
                     func=ACT.Square,
                     scale=inv_sb[:, m : m + 1],
                 )
+
+        def bound_chunk(i):
+            width = OUT_CHUNKS[i]
+            states = slice(starts[i], starts[i] + width)
             result = tile([P, 2, width], F32, "result%d" % i)
-            a, c0 = divmod(start, S // 2)
+            a, c0 = divmod(starts[i], S // 2)
             cap = cap_halves[a][:, :, c0 : c0 + width]
             parts = [slice(0, 1), slice(1, 2)] if width > BLOCK else [slice(0, 2)]
             for part in parts:
                 nc.vector.tensor_tensor(
-                    out=result[:, part, :], in0=squared[:, part, :], in1=cap[:, part, :], op=ALU.min
+                    out=result[:, part, :], in0=squared[i][:, part, :], in1=cap[:, part, :], op=ALU.min
                 )
                 nc.sync.dma_start(out=out.rearrange("(m p) j -> p m j", p=P)[:, part, states], in_=result[:, part, :])
 
-        last = len(OUT_CHUNKS) - 1
-        g_q = [hidden_codes(i) for i in range(last)]
-        output_chunk(0, g_q[0])
-        g_q.append(hidden_codes(last))
-        for i in range(1, last + 1):
-            output_chunk(i, g_q[i])
+        g_chunk(0, relu_scalar)
+        g_chunk(1, relu_scalar)
+        quantize_g(0)
+        g_hid[2] = tile([P, OUT_CHUNKS[2], PACK], BF16, "g_hid2")
+        g_block(2, 0, relu_vector)
+        quantize_g(1)
+        g_block(2, BLOCK, relu_vector)
+        square_chunk(0)
+        g_chunk(3, relu_scalar, "g_q0_codes")
+        g_chunk(4, relu_scalar, "g_q0_plane")
+        bound_chunk(0)
+        for i in range(2, len(OUT_CHUNKS)):
+            quantize_g(i)
+        for i in range(1, len(OUT_CHUNKS)):
+            square_chunk(i)
+            bound_chunk(i)

@@ -23,8 +23,11 @@ BLOCK = 128
 CHUNK = 256
 GATHERS = ([512, 512], [256, 256, 512])
 OUT_CHUNKS = [256, 256, 256, 128, 128]
-EARLY_H = 1
-OUT_BANKS = [0, 1, 2, 3, 4]
+EARLY_H = 2
+G_BANKS = [0, 1, 2, 3, 4, 5, 6, 0]
+OUT_BANKS = [7, 1, 2, 3, 4]
+VECTOR_RELUS = (4, 6)
+W2_SCALAR = 128
 
 
 def tile_picked_yrnd_norm_p_kernel(
@@ -186,7 +189,9 @@ def tile_picked_yrnd_norm_p_kernel(
             quantize_h(c)
 
         src, dst, w2_grouped = second_views(w2_raw, "w2_g")
-        nc.scalar.activation(out=dst, in_=src, func=ACT.Copy)
+        split = W2_SCALAR // 4
+        nc.scalar.activation(out=dst[:, :split], in_=src[:, :split], func=ACT.Copy)
+        nc.vector.tensor_copy(out=dst[:, split:], in_=src[:, split:])
         src, dst, r2_grouped = second_views(r2_raw, "r2_g")
         nc.vector.tensor_scalar(out=dst, in0=src, scalar1=-1.0, scalar2=None, op0=ALU.mult)
         w2_q = quantize(w2_grouped, "w2_q")
@@ -197,16 +202,13 @@ def tile_picked_yrnd_norm_p_kernel(
         g_q = {}
         squared = {}
 
-        def g_chunk(i, relu, tag=None):
-            g_hid[i] = tile([P, OUT_CHUNKS[i], PACK], BF16, "g_hid%d" % i, tag)
+        def g_chunk(i):
+            g_hid[i] = tile([P, OUT_CHUNKS[i], PACK], BF16, "g_hid%d" % i)
             for n0 in range(0, OUT_CHUNKS[i], BLOCK):
-                g_block(i, n0, relu)
-
-        def g_block(i, n0, relu):
-            block = (starts[i] + n0) // BLOCK
-            relu(g_hid[i][:, n0 : n0 + BLOCK, :], first_layer(r1_q, block, bank(block, "g_acc%d" % block)))
-
-        def quantize_g(i):
+                block = (starts[i] + n0) // BLOCK
+                relu = relu_vector if block in VECTOR_RELUS else relu_scalar
+                acc = bank(G_BANKS[block], "g_acc%d" % block)
+                relu(g_hid[i][:, n0 : n0 + BLOCK, :], first_layer(r1_q, block, acc))
             g_q[i] = quantize(g_hid[i][:].rearrange("p n t -> p (n t)"), "g_q%d" % i)
 
         def square_chunk(i):
@@ -249,19 +251,12 @@ def tile_picked_yrnd_norm_p_kernel(
                 )
                 nc.sync.dma_start(out=out.rearrange("(m p) j -> p m j", p=P)[:, part, states], in_=result[:, part, :])
 
-        g_chunk(0, relu_scalar)
-        g_chunk(1, relu_scalar)
-        quantize_g(0)
-        g_hid[2] = tile([P, OUT_CHUNKS[2], PACK], BF16, "g_hid2")
-        g_block(2, 0, relu_vector)
-        quantize_g(1)
-        g_block(2, BLOCK, relu_vector)
+        last = len(OUT_CHUNKS) - 1
+        for i in range(last):
+            g_chunk(i)
         square_chunk(0)
-        g_chunk(3, relu_scalar, "g_q0_codes")
-        g_chunk(4, relu_scalar, "g_q0_plane")
         bound_chunk(0)
-        for i in range(2, len(OUT_CHUNKS)):
-            quantize_g(i)
-        for i in range(1, len(OUT_CHUNKS)):
+        g_chunk(last)
+        for i in range(1, last + 1):
             square_chunk(i)
             bound_chunk(i)

@@ -21,13 +21,12 @@ PACK = 4
 PASSES = K // (P * PACK)
 BLOCK = 128
 CHUNK = 256
-GATHERS = ([512, 512], [256, 256, 512])
+GATHERS = ([1024], [256, 256, 512])
 OUT_CHUNKS = [256, 256, 256, 128, 128]
 EARLY_H = 2
 G_BANKS = [0, 1, 2, 3, 4, 5, 6, 0]
 OUT_BANKS = [7, 1, 2, 3, 4]
 VECTOR_RELUS = (4, 6)
-W2_SCALAR = 128
 
 
 def tile_picked_yrnd_norm_p_kernel(
@@ -58,23 +57,22 @@ def tile_picked_yrnd_norm_p_kernel(
         def move_scales(o):
             for r in range(4):
                 nc.sync.dma_start(
-                    out=x_planes[o][r:P:32, :].bitcast(I32),
+                    out=x_plane[r:P:32, o * S : (o + 1) * S].bitcast(I32),
                     in_=picked_scales[64 * o + 4 * r : 64 * o + 64 : 16, :].bitcast(I32),
                 )
 
         offsets = keep.tile([P, S // 16], U16, name="offsets")
         scale_table = tile([P, T], U8, "scale_table")
         nc.vector.memset(scale_table[:].bitcast(I32), 0)
-        x_planes = [tile([P, S], U8, "x_plane%d" % o) for o in range(PASSES)]
-        for plane in x_planes:
-            nc.vector.memset(plane[:].bitcast(I32), 0)
+        x_plane = tile([P, PASSES * S], U8, "x_plane")
+        nc.vector.memset(x_plane[:].bitcast(I32), 0)
         inv_rows = tile([P, P], F32, "inv_rows")
         nc.gpsimd.memset(inv_rows[:], 0.0)
         identity = tile([P, P], F32, "identity")
         make_identity(nc, identity[:])
 
         nc.sync.dma_start(offsets[:], offs)
-        w1_raw = [None, load_rows(w1, 512, H, "w1_raw1")]
+        w1_raw = [load_rows(w1, 0, H, "w1_raw0")]
         nc.sync.dma_start(
             out=scale_table[0:P:4, :].bitcast(I32), in_=x_scales.rearrange("o q c -> (o q) c").bitcast(I32)
         )
@@ -84,7 +82,7 @@ def tile_picked_yrnd_norm_p_kernel(
         inv_sb = tile([P, 2], F32, "inv_sb")
         nc.scalar.copy(out=inv_sb[:], in_=turned[:, 0:2])
         word_tables = [load_words(0)]
-        w1_raw[0] = load_rows(w1, 0, H, "w1_raw0")
+        w1_raw.append(load_rows(w1, 512, H, "w1_raw1"))
         picked_scales = tile([P, S], U8, "picked_scales")
         nc.vector.tensor_copy(out=picked_scales[:], in_=scale_table[:].indirect(offsets[:]))
         move_scales(0)
@@ -118,17 +116,24 @@ def tile_picked_yrnd_norm_p_kernel(
             nc.vector.quantize_mx(out=codes[:].bitcast(FP8X4), scales=plane[:], in_=grouped)
             return codes, plane
 
-        def first_weights(raw, name, tag=None, scalar_second=False):
+        def whole_pass(raw, name, on_scalar):
+            g = tile([P, PACK, P, PACK], BF16, name + "_g")
+            src = raw[:].rearrange("p j (m t) -> p m j t", t=PACK)
+            dst = g[:].rearrange("p t m j -> p m j t")
+            if on_scalar:
+                for t in range(PACK):
+                    nc.scalar.activation(out=dst[:, :, :, t], in_=src[:, :, :, t], func=ACT.Copy)
+            else:
+                nc.vector.tensor_copy(out=dst, in_=src)
+            codes, plane = quantize(g[:].rearrange("p t m j -> p (t m j)"), name + "_q")
+            return [(codes[:, t * P : (t + 1) * P], plane[:, t * P : (t + 1) * P]) for t in range(PACK)]
+
+        def first_weights(raw, name):
             grouped = []
             for u in range(2):
-                g = tile([P, 2, P, PACK], BF16, "%s_g%d" % (name, u), tag if u == 0 else None)
+                g = tile([P, 2, P, PACK], BF16, "%s_g%d" % (name, u))
                 src = raw[:].rearrange("p j (m u e) -> p u m j e", u=2, e=2)[:, u]
-                dst = g[:].rearrange("p e m j -> p m j e")
-                if scalar_second and u == 1:
-                    for e in range(2):
-                        nc.scalar.activation(out=dst[:, :, :, e], in_=src[:, :, :, e], func=ACT.Copy)
-                else:
-                    nc.vector.tensor_copy(out=dst, in_=src)
+                nc.vector.tensor_copy(out=g[:].rearrange("p e m j -> p m j e"), in_=src)
                 grouped.append(g)
             slots = []
             for u in range(2):
@@ -151,7 +156,7 @@ def tile_picked_yrnd_norm_p_kernel(
                         lhsT=codes.bitcast(FP8X4),
                         lhsT_scale=plane,
                         rhs=x_codes[o][block].bitcast(FP8X4),
-                        rhs_scale=x_planes[o][:, block * BLOCK : (block + 1) * BLOCK],
+                        rhs_scale=x_plane[:, o * S + block * BLOCK : o * S + (block + 1) * BLOCK],
                         start=(o == 0 and t == 0),
                         stop=(o == PASSES - 1 and t == PACK - 1),
                     )
@@ -163,7 +168,7 @@ def tile_picked_yrnd_norm_p_kernel(
         def relu_vector(dst, src):
             nc.vector.tensor_scalar(out=dst, in0=src, scalar1=0.0, scalar2=None, op0=ALU.max)
 
-        w1_q = [first_weights(w1_raw[0], "w1_0"), first_weights(w1_raw[1], "w1_1", "scale_table", True)]
+        w1_q = [whole_pass(w1_raw[0], "w1_0", True), whole_pass(w1_raw[1], "w1_1", False)]
         h_hid = []
         for c in range(S // CHUNK):
             grouped = tile([P, CHUNK, PACK], BF16, "h_hid%d" % c)
@@ -189,9 +194,7 @@ def tile_picked_yrnd_norm_p_kernel(
             quantize_h(c)
 
         src, dst, w2_grouped = second_views(w2_raw, "w2_g")
-        split = W2_SCALAR // 4
-        nc.scalar.activation(out=dst[:, :split], in_=src[:, :split], func=ACT.Copy)
-        nc.vector.tensor_copy(out=dst[:, split:], in_=src[:, split:])
+        nc.scalar.activation(out=dst, in_=src, func=ACT.Copy)
         src, dst, r2_grouped = second_views(r2_raw, "r2_g")
         nc.vector.tensor_scalar(out=dst, in0=src, scalar1=-1.0, scalar2=None, op0=ALU.mult)
         w2_q = quantize(w2_grouped, "w2_q")

@@ -21,9 +21,9 @@ PACK = 4
 PASSES = K // (P * PACK)
 BLOCK = 128
 CHUNK = 256
-GATHERS = ([1024], [256, 256, 512])
+GATHERS = ([1024], [512, 512])
 OUT_CHUNKS = [256, 256, 256, 128, 128]
-EARLY_H = 2
+EARLY_H = 1
 G_BANKS = [0, 1, 2, 3, 4, 5, 6, 0]
 OUT_BANKS = [7, 1, 2, 3, 4]
 VECTOR_RELUS = (4, 6)

@@ -38,7 +38,7 @@ def tile_picked_yrnd_norm_p_kernel(
         psum = ctx.enter_context(tc.psum_pool(name="psum", bufs=1))
 
         def tile(shape, dtype, name, tag=None):
-            return keep.tile(shape, dtype, name=name, tag=tag or name, align_bytes=64)
+            return keep.tile(shape, dtype, name=name, tag=tag or name, align_bytes=256)
 
         def bank(index, name):
             return psum.tile([P, 512], F32, name=name, tag="bank%d" % index)
@@ -71,12 +71,12 @@ def tile_picked_yrnd_norm_p_kernel(
         identity = tile([P, P], F32, "identity")
         make_identity(nc, identity[:])
 
-        nc.sync.dma_start(offsets[:], offs)
         w1_raw = [load_rows(w1, 0, H, "w1_raw0")]
+        nc.sync.dma_start(offsets[:], offs)
         nc.sync.dma_start(
             out=scale_table[0:P:4, :].bitcast(I32), in_=x_scales.rearrange("o q c -> (o q) c").bitcast(I32)
         )
-        nc.sync.dma_start(out=inv_rows[0:2, :], in_=inv.rearrange("(m p) u -> m (p u)", p=P))
+        nc.scalar.dma_start(out=inv_rows[0:2, :], in_=inv.rearrange("(m p) u -> m (p u)", p=P))
         turned = bank(7, "turned")
         nc.tensor.transpose(turned[:, 0:P], inv_rows[:], identity[:])
         inv_sb = tile([P, 2], F32, "inv_sb")

@@ -24,6 +24,7 @@ CHUNK = 256
 GATHERS = ([1024], [512, 512])
 OUT_CHUNKS = [256, 256, 256, 128, 128]
 EARLY_H = 1
+PLANE_ROW = (0, 4)
 G_BANKS = [0, 1, 2, 3, 4, 5, 6, 0]
 OUT_BANKS = [7, 1, 2, 3, 4]
 VECTOR_RELUS = (4, 6)
@@ -57,7 +58,7 @@ def tile_picked_yrnd_norm_p_kernel(
         def move_scales(o):
             for r in range(4):
                 nc.sync.dma_start(
-                    out=x_plane[r:P:32, o * S : (o + 1) * S].bitcast(I32),
+                    out=x_plane[PLANE_ROW[o] + r : P : 32, o * S : (o + 1) * S].bitcast(I32),
                     in_=picked_scales[64 * o + 4 * r : 64 * o + 64 : 16, :].bitcast(I32),
                 )
 
@@ -156,7 +157,7 @@ def tile_picked_yrnd_norm_p_kernel(
                         lhsT=codes.bitcast(FP8X4),
                         lhsT_scale=plane,
                         rhs=x_codes[o][block].bitcast(FP8X4),
-                        rhs_scale=x_plane[:, o * S + block * BLOCK : o * S + (block + 1) * BLOCK],
+                        rhs_scale=x_plane[PLANE_ROW[o] :, o * S + block * BLOCK : o * S + (block + 1) * BLOCK],
                         start=(o == 0 and t == 0),
                         stop=(o == PASSES - 1 and t == PACK - 1),
                     )

@@ -21,7 +21,7 @@ PACK = 4
 PASSES = K // (P * PACK)
 BLOCK = 128
 CHUNK = 256
-GATHERS = ([1024], [512, 512])
+GATHERS = ([1024], [384, 640])
 OUT_CHUNKS = [256, 256, 256, 128, 128]
 EARLY_H = 1
 PLANE_ROW = (0, 4)

@@ -24,7 +24,8 @@ CHUNK = 256
 GATHERS = ([1024], [384, 640])
 OUT_CHUNKS = [256, 256, 256, 128, 128]
 EARLY_H = 1
-PLANE_ROW = (0, 4)
+PLANE_ROW = (8, 4)
+HIDDEN_ROW = 4
 G_BANKS = [0, 1, 2, 3, 4, 5, 6, 0]
 OUT_BANKS = [7, 1, 2, 3, 4]
 VECTOR_RELUS = (4, 6)
@@ -110,11 +111,11 @@ def tile_picked_yrnd_norm_p_kernel(
                 x_codes[o].extend(codes[:, c : c + BLOCK] for c in range(0, width, BLOCK))
                 start = start + width
 
-        def quantize(grouped, name):
+        def quantize(grouped, name, row=0):
             width = grouped.shape[1] // PACK
             codes = tile([P, width], U32, name + "_codes")
-            plane = tile([P, width], U8, name + "_plane")
-            nc.vector.quantize_mx(out=codes[:].bitcast(FP8X4), scales=plane[:], in_=grouped)
+            plane = tile([P, width], U8, name + "_plane")[row:, :]
+            nc.vector.quantize_mx(out=codes[:].bitcast(FP8X4), scales=plane, in_=grouped)
             return codes, plane
 
         def whole_pass(raw, name, on_scalar):
@@ -183,7 +184,7 @@ def tile_picked_yrnd_norm_p_kernel(
 
         def quantize_h(c):
             cols = slice(c * CHUNK, (c + 1) * CHUNK)
-            nc.vector.quantize_mx(out=h_codes[:, cols].bitcast(FP8X4), scales=h_planes[-1][:, cols], in_=h_hid[c])
+            nc.vector.quantize_mx(out=h_codes[:, cols].bitcast(FP8X4), scales=h_planes[-1][HIDDEN_ROW:, cols], in_=h_hid[c])
 
         r1_q = [first_weights(r1_raw[0], "r1_0")]
         h_planes.append(tile([P, S], U8, "h_plane_early", "r1_0_g0"))
@@ -213,13 +214,13 @@ def tile_picked_yrnd_norm_p_kernel(
                 relu = relu_vector if block in VECTOR_RELUS else relu_scalar
                 acc = bank(G_BANKS[block], "g_acc%d" % block)
                 relu(g_hid[i][:, n0 : n0 + BLOCK, :], first_layer(r1_q, block, acc))
-            g_q[i] = quantize(g_hid[i][:].rearrange("p n t -> p (n t)"), "g_q%d" % i)
+            g_q[i] = quantize(g_hid[i][:].rearrange("p n t -> p (n t)"), "g_q%d" % i, HIDDEN_ROW)
 
         def square_chunk(i):
             width = OUT_CHUNKS[i]
             states = slice(starts[i], starts[i] + width)
             h_plane = h_planes[0 if starts[i] < EARLY_H * CHUNK else 1]
-            products = ((w2_q, h_codes[:, states], h_plane[:, states]), (r2_q, g_q[i][0][:], g_q[i][1][:]))
+            products = ((w2_q, h_codes[:, states], h_plane[HIDDEN_ROW:, states]), (r2_q, g_q[i][0][:], g_q[i][1]))
             acc = bank(OUT_BANKS[i], "out_acc%d" % i)
             for j, (weights, codes, plane) in enumerate(products):
                 for m in range(2):

from contextlib import ExitStack

import concourse.mybir as mybir
from concourse.masks import make_identity

K, T, S, H, N = 1024, 4096, 1024, 512, 256
FLOPS = 2 * S * (2 * K * H + 2 * H * N)

F32 = mybir.dt.float32
BF16 = mybir.dt.bfloat16
I32 = mybir.dt.int32
U32 = mybir.dt.uint32
U16 = mybir.dt.uint16
U8 = mybir.dt.uint8
FP8X4 = mybir.dt.float8_e4m3fn_x4
ACT = mybir.ActivationFunctionType
ALU = mybir.AluOpType

P = 128
PACK = 4
PASSES = K // (P * PACK)
BLOCK = 128
CHUNK = 256
GATHERS = ([1024], [384, 640])
OUT_CHUNKS = [256, 256, 256, 128, 128]
EARLY_H = 1
PLANE_ROW = (8, 4)
HIDDEN_ROW = 4
G_BANKS = [0, 1, 2, 3, 4, 5, 6, 0]
OUT_BANKS = [7, 1, 2, 3, 4]
VECTOR_RELUS = (4, 6)


def tile_picked_yrnd_norm_p_kernel(
    tc, x_words, x_scales, w1, r1, w2, r2, inv, capv, offs, out
):
    nc = tc.nc
    with ExitStack() as ctx:
        keep = ctx.enter_context(tc.tile_pool(name="keep", bufs=1))
        psum = ctx.enter_context(tc.psum_pool(name="psum", bufs=1))

        def tile(shape, dtype, name, tag=None):
            return keep.tile(shape, dtype, name=name, tag=tag or name, align_bytes=256)

        def bank(index, name):
            return psum.tile([P, 512], F32, name=name, tag="bank%d" % index)

        def load_rows(w, first_row, width, name):
            raw = tile([P, PACK, width], F32, name)
            rows = w[first_row : first_row + P * PACK, :]
            nc.sync.dma_start(out=raw[:], in_=rows.rearrange("(p j) c -> p j c", j=PACK))
            return raw

        def load_words(o):
            table = tile([P, T], I32, "word_table%d" % o)
            nc.sync.dma_start(out=table[:], in_=x_words[o].rearrange("p c r -> p (c r)").bitcast(I32))
            return table

        def move_scales(o):
            for r in range(4):
                nc.sync.dma_start(
                    out=x_plane[PLANE_ROW[o] + r : P : 32, o * S : (o + 1) * S].bitcast(I32),
                    in_=picked_scales[64 * o + 4 * r : 64 * o + 64 : 16, :].bitcast(I32),
                )

        offsets = keep.tile([P, S // 16], U16, name="offsets")
        scale_table = tile([P, T], U8, "scale_table")
        nc.vector.memset(scale_table[:].bitcast(I32), 0)
        x_plane = tile([P, PASSES * S], U8, "x_plane")
        nc.vector.memset(x_plane[:].bitcast(I32), 0)
        inv_rows = tile([P, P], F32, "inv_rows")
        nc.gpsimd.memset(inv_rows[:], 0.0)
        identity = tile([P, P], F32, "identity")
        make_identity(nc, identity[:])

        w1_raw = [load_rows(w1, 0, H, "w1_raw0")]
        nc.sync.dma_start(offsets[:], offs)
        nc.sync.dma_start(
            out=scale_table[0:P:4, :].bitcast(I32), in_=x_scales.rearrange("o q c -> (o q) c").bitcast(I32)
        )
        nc.scalar.dma_start(out=inv_rows[0:2, :], in_=inv.rearrange("(m p) u -> m (p u)", p=P))
        turned = bank(7, "turned")
        nc.tensor.transpose(turned[:, 0:P], inv_rows[:], identity[:])
        inv_sb = tile([P, 2], F32, "inv_sb")
        nc.scalar.copy(out=inv_sb[:], in_=turned[:, 0:2])
        word_tables = [load_words(0)]
        w1_raw.append(load_rows(w1, 512, H, "w1_raw1"))
        picked_scales = tile([P, S], U8, "picked_scales")
        nc.vector.tensor_copy(out=picked_scales[:], in_=scale_table[:].indirect(offsets[:]))
        move_scales(0)
        word_tables.append(load_words(1))
        move_scales(1)
        r1_raw = [load_rows(r1, 512 * o, H, "r1_raw%d" % o) for o in range(PASSES)]
        w2_raw = load_rows(w2, 0, N, "w2_raw")
        r2_raw = load_rows(r2, 0, N, "r2_raw")
        cap_halves = []
        for a in range(2):
            cap_sb = tile([P, 2, S // 2], F32, "cap_sb%d" % a)
            nc.sync.dma_start(
                out=cap_sb[:], in_=capv.rearrange("(m p) j -> p m j", p=P)[:, :, a * (S // 2) : (a + 1) * (S // 2)]
            )
            cap_halves.append(cap_sb)

        x_codes = [[], []]
        for o in range(PASSES):
            start = 0
            for width in GATHERS[o]:
                codes = tile([P, width], U32, "x_codes%d_%d" % (o, start))
                picks = offsets[:, start // 16 : (start + width) // 16]
                nc.vector.tensor_copy(out=codes[:], in_=word_tables[o][:].bitcast(U32).indirect(picks))
                x_codes[o].extend(codes[:, c : c + BLOCK] for c in range(0, width, BLOCK))
                start = start + width

        def quantize(grouped, name, row=0):
            width = grouped.shape[1] // PACK
            codes = tile([P, width], U32, name + "_codes")
            plane = tile([P, width], U8, name + "_plane")[row:, :]
            nc.vector.quantize_mx(out=codes[:].bitcast(FP8X4), scales=plane, in_=grouped)
            return codes, plane

        def whole_pass(raw, name, on_scalar):
            g = tile([P, PACK, P, PACK], BF16, name + "_g")
            src = raw[:].rearrange("p j (m t) -> p m j t", t=PACK)
            dst = g[:].rearrange("p t m j -> p m j t")
            if on_scalar:
                for t in range(PACK):
                    nc.scalar.activation(out=dst[:, :, :, t], in_=src[:, :, :, t], func=ACT.Copy)
            else:
                nc.vector.tensor_copy(out=dst, in_=src)
            codes, plane = quantize(g[:].rearrange("p t m j -> p (t m j)"), name + "_q")
            return [(codes[:, t * P : (t + 1) * P], plane[:, t * P : (t + 1) * P]) for t in range(PACK)]

        def first_weights(raw, name):
            grouped = []
            for u in range(2):
                g = tile([P, 2, P, PACK], BF16, "%s_g%d" % (name, u))
                src = raw[:].rearrange("p j (m u e) -> p u m j e", u=2, e=2)[:, u]
                nc.vector.tensor_copy(out=g[:].rearrange("p e m j -> p m j e"), in_=src)
                grouped.append(g)
            slots = []
            for u in range(2):
                codes, plane = quantize(grouped[u][:].rearrange("p e m j -> p (e m j)"), "%s_q%d" % (name, u))
                slots.extend((codes[:, e * P : (e + 1) * P], plane[:, e * P : (e + 1) * P]) for e in range(2))
            return slots

        def second_views(raw, name):
            g = tile([P, N, PACK], BF16, name)
            src = raw[:].rearrange("p t (c i) -> p c t i", i=4)
            dst = g[:].rearrange("p (c i) t -> p c t i", i=4)
            return src, dst, g[:].rearrange("p n t -> p (n t)")

        def first_layer(weights, block, acc):
            for o in range(PASSES):
                for t in range(PACK):
                    codes, plane = weights[o][t]
                    nc.tensor.matmul_mx(
                        out=acc[:, t * BLOCK : (t + 1) * BLOCK],
                        lhsT=codes.bitcast(FP8X4),
                        lhsT_scale=plane,
                        rhs=x_codes[o][block].bitcast(FP8X4),
                        rhs_scale=x_plane[PLANE_ROW[o] :, o * S + block * BLOCK : o * S + (block + 1) * BLOCK],
                        start=(o == 0 and t == 0),
                        stop=(o == PASSES - 1 and t == PACK - 1),
                    )
            return acc[:].rearrange("p (t n) -> p n t", t=PACK)

        def relu_scalar(dst, src):
            nc.scalar.activation(out=dst, in_=src, func=ACT.Relu)

        def relu_vector(dst, src):
            nc.vector.tensor_scalar(out=dst, in0=src, scalar1=0.0, scalar2=None, op0=ALU.max)

        w1_q = [whole_pass(w1_raw[0], "w1_0", True), whole_pass(w1_raw[1], "w1_1", False)]
        h_hid = []
        for c in range(S // CHUNK):
            grouped = tile([P, CHUNK, PACK], BF16, "h_hid%d" % c)
            for n0 in range(0, CHUNK, BLOCK):
                block = (c * CHUNK + n0) // BLOCK
                relu_scalar(grouped[:, n0 : n0 + BLOCK, :], first_layer(w1_q, block, bank(block, "h_acc%d" % block)))
            h_hid.append(grouped[:].rearrange("p n t -> p (n t)"))

        h_codes = tile([P, S], U32, "h_codes")
        h_planes = []

        def quantize_h(c):
            cols = slice(c * CHUNK, (c + 1) * CHUNK)
            nc.vector.quantize_mx(out=h_codes[:, cols].bitcast(FP8X4), scales=h_planes[-1][HIDDEN_ROW:, cols], in_=h_hid[c])

        r1_q = [first_weights(r1_raw[0], "r1_0")]
        h_planes.append(tile([P, S], U8, "h_plane_early", "r1_0_g0"))
        for c in range(EARLY_H):
            quantize_h(c)
        r1_q.append(first_weights(r1_raw[1], "r1_1"))
        h_planes.append(tile([P, S], U8, "h_plane_late", "r1_1_g0"))
        for c in range(EARLY_H, S // CHUNK):
            quantize_h(c)

        src, dst, w2_grouped = second_views(w2_raw, "w2_g")
        nc.scalar.activation(out=dst, in_=src, func=ACT.Copy)
        src, dst, r2_grouped = second_views(r2_raw, "r2_g")
        nc.vector.tensor_scalar(out=dst, in0=src, scalar1=-1.0, scalar2=None, op0=ALU.mult)
        w2_q = quantize(w2_grouped, "w2_q")
        r2_q = quantize(r2_grouped, "r2_q")

        starts = [sum(OUT_CHUNKS[:i]) for i in range(len(OUT_CHUNKS))]
        g_hid = {}
        g_q = {}
        squared = {}

        def g_chunk(i):
            g_hid[i] = tile([P, OUT_CHUNKS[i], PACK], BF16, "g_hid%d" % i)
            for n0 in range(0, OUT_CHUNKS[i], BLOCK):
                block = (starts[i] + n0) // BLOCK
                relu = relu_vector if block in VECTOR_RELUS else relu_scalar
                acc = bank(G_BANKS[block], "g_acc%d" % block)
                relu(g_hid[i][:, n0 : n0 + BLOCK, :], first_layer(r1_q, block, acc))
            g_q[i] = quantize(g_hid[i][:].rearrange("p n t -> p (n t)"), "g_q%d" % i, HIDDEN_ROW)

        def square_chunk(i):
            width = OUT_CHUNKS[i]
            states = slice(starts[i], starts[i] + width)
            h_plane = h_planes[0 if starts[i] < EARLY_H * CHUNK else 1]
            products = ((w2_q, h_codes[:, states], h_plane[HIDDEN_ROW:, states]), (r2_q, g_q[i][0][:], g_q[i][1]))
            acc = bank(OUT_BANKS[i], "out_acc%d" % i)
            for j, (weights, codes, plane) in enumerate(products):
                for m in range(2):
                    rows = slice(m * P, (m + 1) * P)
                    nc.tensor.matmul_mx(
                        out=acc[:, m * width : (m + 1) * width],
                        lhsT=weights[0][:, rows].bitcast(FP8X4),
                        lhsT_scale=weights[1][:, rows],
                        rhs=codes.bitcast(FP8X4),
                        rhs_scale=plane,
                        start=(j == 0 and m == 0),
                        stop=(j == 1 and m == 1),
                    )
            squared[i] = tile([P, 2, width], F32, "squared%d" % i)
            for m in range(2):
                nc.scalar.activation(
                    out=squared[i][:, m, :],
                    in_=acc[:, m * width : (m + 1) * width],
                    func=ACT.Square,
                    scale=inv_sb[:, m : m + 1],
                )

        def bound_chunk(i):
            width = OUT_CHUNKS[i]
            states = slice(starts[i], starts[i] + width)
            result = tile([P, 2, width], F32, "result%d" % i)
            a, c0 = divmod(starts[i], S // 2)
            cap = cap_halves[a][:, :, c0 : c0 + width]
            parts = [slice(0, 1), slice(1, 2)] if width > BLOCK else [slice(0, 2)]
            for part in parts:
                nc.vector.tensor_tensor(
                    out=result[:, part, :], in0=squared[i][:, part, :], in1=cap[:, part, :], op=ALU.min
                )
                nc.sync.dma_start(out=out.rearrange("(m p) j -> p m j", p=P)[:, part, states], in_=result[:, part, :])

        last = len(OUT_CHUNKS) - 1
        for i in range(last):
            g_chunk(i)
        square_chunk(0)
        bound_chunk(0)
        g_chunk(last)
        for i in range(1, last + 1):
            square_chunk(i)
            bound_chunk(i)
